import numpy as np, ml_dtypes
CORES = [29,45,93,109,157,173,221,237,285,301,349,365,413,429,477,493]
N = 16
import mx_ref
KO = 1
F = np.float32(0.8)
OWN = [5,6,7,12,14,5,6,7,5,6,7,12,12,14,14,5]
BF = ml_dtypes.bfloat16
def tile(rs):
    return np.stack(rs, axis=2).reshape(128, -1).astype(BF)
def pick(b):
    s = np.zeros((128, 128, 4), np.float32)
    s[np.arange(128), np.arange(128), b] = 1.0
    return mx_ref.quantize(s.reshape(128, 512).astype(BF))
def pk(c, s, i=0):
    return (np.ascontiguousarray(c[:, 512 * i:512 * i + 512]), mx_ref.live(s[:, 128 * i:128 * i + 128]))
def inputs(rng, e, E):
    def f(*shape):
        v = (rng.standard_normal(shape, dtype=np.float32) * np.exp2(rng.integers(-2, 3, shape[:-1] + (1,)))).astype(BF)
        return mx_ref.spread((v.astype(np.float32) * np.exp2(rng.integers(-E, E + 1, shape[:-2] + (1, 1))).astype(np.float32)).astype(BF), rng, e)
    def packed(k):
        c = np.zeros((N, 128, k * 512), np.uint8); s = np.zeros((N, 128, k * 128), np.uint8)
        for r in range(N):
            for i in range(k):
                a, b = mx_ref.quantize(f(128, 512)); c[r][:, 512 * i:512 * i + 512] = a; s[r][:, 128 * i:128 * i + 128] = mx_ref.plane(b, rng)
        return c, s
    d = {}
    d["kc"], d["ks"] = packed(KO)
    d["q"] = f(N, 128, 512)
    return d
def setup_inputs(rng):
    return inputs(rng, 0, 0)
def setup_inputs_blocks(rng):
    return inputs(rng, 4, 0)
def setup_inputs_wide(rng):
    return inputs(rng, 0, 8)
def reference(kc, ks, q):
    S = [pick(t) for t in range(4)]
    anew = lambda p, i: mx_ref.quantize(tile([mx_ref.matmul(S[t], pk(kc[p], ks[p], i)) * F for t in range(4)]))
    y = np.full((N, 128, 512), np.nan, np.float32)
    for o in range(N):
        if OWN[o] != o: continue
        qq = mx_ref.quantize(q[o])
        M = [pk(kc[o], ks[o], i) for i in range(KO)] + [anew(p, i) for p in range(N) if p != o and OWN[p] == o for i in range(KO)]
        y[o][:, :128 * len(M)] = np.concatenate([mx_ref.matmul(qq, m) for m in M], axis=1)
    return {"y": y}

@@ -1,0 +1,155 @@
+import numpy as np
+from concourse.bass import DstId, RemoteDMATransfer
+from concourse.mybir import dt, AluOpType, ActivationFunctionType
+
+W = 128
+SCRATCH = {
+    "mc": ("sbuf", [128, 4 * W], "float8_e4m3fn_x4"),
+    "ms": ("sbuf", [128, 4 * W], "uint8"),
+    "ndiag": ("sbuf", [128, W], "bfloat16"),
+    "z": ("sbuf", [128, 4 * W + 4], "bfloat16"),
+    "sc": ("sbuf", [128, 4 * W], "float8_e4m3fn_x4"),
+    "ss": ("sbuf", [128, 4 * W], "uint8"),
+    "kt": ("sbuf", [128, 4 * W], "bfloat16"),
+    "nc": ("sbuf", [128, W], "float8_e4m3fn_x4"),
+    "ns": ("sbuf", [128, W], "uint8"),
+    "rc": ("sbuf", [128, W], "float8_e4m3fn_x4"),
+    "rs": ("sbuf", [128, W], "uint8"),
+    "qt": ("sbuf", [128, 4 * W], "bfloat16"),
+    "qc": ("sbuf", [128, W], "float8_e4m3fn_x4"),
+    "qs": ("sbuf", [128, W], "uint8"),
+    "yt": ("sbuf", [128, 4 * W], "float32"),
+    "ps": ("psum", [128, 2048], "float32"),
+}
+SEMAPHORES = (["ldk", "ldq", "zero", "iota", "diag", "sq", "scaled", "kq", "snd", "relc", "rels", "qq", "st"]
+              + ["mm%d" % i for i in range(4)] + ["arr%d" % i for i in range(4)] + ["cp%d" % i for i in range(4)])
+F = float(np.float32(0.8))
+
+
+def plan(T, topo):
+    own, cores = T.tables["OWN"], T.cores
+    n = len(own)
+    prods = {o: [p for p in range(n) if own[p] == o and p != o] for o in range(n) if own[o] == o}
+    codes_by, plane_by = {}, {}
+    for o in prods:
+        for p in prods[o]:
+            a, b = cores[p], cores[o]
+            if topo.may_write(a, b):
+                continue
+            ok = [r for r in range(n) if own[r] != r and topo.may_write(a, cores[r]) and topo.may_write(cores[r], b)]
+            first = [r for r in ok if topo.chip(cores[r]) == topo.chip(a) and topo.same_plane(cores[r], b)]
+            second = [r for r in ok if topo.chip(cores[r]) == topo.chip(b) and topo.same_plane(a, cores[r])]
+            first, second = first or ok, second or ok
+            codes_by[p] = first[0]
+            plane_by[p] = second[0]
+    return prods, codes_by, plane_by
+
+
+def bits(m):
+    return bin(m).count("1")
+
+
+def rank_program(g, core, T, topo):
+    rank = T.rank_of(core)
+    if rank is None:
+        return
+    own, cores, sem = T.tables["OWN"], T.cores, T.sem
+    prods, codes_by, plane_by = plan(T, topo)
+    slot = {p: 1 + i for o in prods for i, p in enumerate(prods[o])}
+
+    def cols(b):
+        return slice(W * b, W * b + W)
+
+    def bank(b):
+        return T.ps[:, 512 * b:512 * b + W]
+
+    def codes(ap):
+        return ap.bitcast(dt.uint8)
+
+    if own[rank] == rank:
+        g.sync.dma_start(T.qt[:], T.q[:]).then_inc(sem.ldq, 16)
+        g.scalar.dma_start(codes(T.mc[:, cols(0)]), T.kc[:]).then_inc(sem.ldk, 16)
+        g.sync.dma_start(T.ms[:, cols(0)], T.ks[:]).then_inc(sem.ldk, 16)
+        g.vector.wait_ge(sem.ldq, 16)
+        g.vector.quantize_mx(T.qc[:], T.qs[:], T.qt[:]).then_inc(sem.qq, 1)
+        g.tensor.wait_ge(sem.qq, 1)
+
+        def lateness(p):
+            if p in codes_by:
+                return 2
+            return 0 if topo.rack(topo.host(cores[p])) == topo.rack(topo.host(core)) else 1
+        order = [rank] + sorted(prods[rank], key=lateness)
+        for i, p in enumerate(order):
+            s = 0 if p == rank else slot[p]
+            if p == rank:
+                g.tensor.wait_ge(sem.ldk, 32)
+            else:
+                mc = topo.mask(cores[codes_by.get(p, p)], core)
+                ms = topo.mask(cores[plane_by.get(p, p)], core)
+                g.tensor.wait_ge(sem["arr%d" % s], bits(mc) + bits(ms))
+            mm, cp = sem["mm%d" % s], sem["cp%d" % s]
+            g.tensor.matmul_mx(bank(s), T.qc[:], T.qs[:], T.mc[:, cols(s)], T.ms[:, cols(s)], True, True).then_inc(mm, 1)
+            if (len(order) - 1 - i) % 2 == 0:
+                g.vector.wait_ge(mm, 1)
+                g.vector.tensor_copy(T.yt[:, cols(s)], bank(s)).then_inc(cp, 1)
+                dq = g.sync
+            else:
+                g.scalar.wait_ge(mm, 1)
+                g.scalar.activation(T.yt[:, cols(s)], bank(s), ActivationFunctionType.Copy).then_inc(cp, 1)
+                dq = g.scalar
+            dq.wait_ge(cp, 1)
+            dq.dma_start(T.y[:, cols(s)], T.yt[:, cols(s)]).then_inc(sem.st, 16)
+        g.sync.wait_ge(sem.st, 16 * len(order))
+        return
+
+    g.sync.dma_start(codes(T.mc[:, cols(0)]), T.kc[:]).then_inc(sem.ldk, 16)
+    g.scalar.dma_start(T.ms[:, cols(0)], T.ks[:]).then_inc(sem.ldk, 16)
+    g.iota(T.ndiag[:], [[1, W]], 0, -1, allow_small_or_imprecise_dtypes=True).then_inc(sem.iota, 1)
+    g.vector.memset(T.z[:], 0.0).then_inc(sem.zero, 1)
+    g.vector.wait_ge(sem.zero, 1)
+    g.vector.wait_ge(sem.iota, 1)
+    g.vector.tensor_scalar(T.z[:, 3:4 * W:4], T.ndiag[:], 0.0, None, AluOpType.is_equal).then_inc(sem.diag, 1)
+    g.vector.wait_ge(sem.diag, 1)
+    for b in range(4):
+        g.vector.quantize_mx(T.sc[:, cols(b)], T.ss[:, cols(b)], T.z[:, 3 - b:3 - b + 4 * W]).then_inc(sem.sq, 1)
+    g.tensor.wait_ge(sem.sq, 4)
+    g.tensor.wait_ge(sem.ldk, 32)
+    for b in range(4):
+        g.tensor.matmul_mx(bank(b), T.sc[:, cols(b)], T.ss[:, cols(b)], T.mc[:, cols(0)], T.ms[:, cols(0)],
+                           True, True).then_inc(sem["mm%d" % b], 1)
+    for b in range(4):
+        out = T.kt[:, b:4 * W:4]
+        if b % 2 == 0:
+            g.scalar.wait_ge(sem["mm%d" % b], 1)
+            g.scalar.activation(out, bank(b), ActivationFunctionType.Copy, scale=F).then_inc(sem.scaled, 1)
+        else:
+            g.vector.wait_ge(sem["mm%d" % b], 1)
+            g.vector.tensor_scalar(out, bank(b), F, None, AluOpType.mult).then_inc(sem.scaled, 1)
+    g.vector.wait_ge(sem.scaled, 4)
+    g.vector.quantize_mx(T.nc[:], T.ns[:], T.kt[:]).then_inc(sem.kq, 1)
+
+    sent = [0]
+
+    def send(out, in_, rsem, dst):
+        rid, pid = topo.addr(dst, core)
+        m = topo.mask(core, dst)
+        g.remote_dma(out, in_, rsem, sem.snd, pid, rid, m)
+        sent[0] += bits(m)
+
+    g.wait_ge(sem.kq, 1)
+    s, o = slot[rank], own[rank]
+    if rank in codes_by:
+        send(codes(T.rc[:]), codes(T.nc[:]), sem.relc, cores[codes_by[rank]])
+        send(T.rs[:], T.ns[:], sem.rels, cores[plane_by[rank]])
+    else:
+        send(codes(T.mc[:, cols(s)]), codes(T.nc[:]), sem["arr%d" % s], cores[o])
+        send(T.ms[:, cols(s)], T.ns[:], sem["arr%d" % s], cores[o])
+    for p in sorted(codes_by):
+        so, oo = slot[p], own[p]
+        if codes_by[p] == rank:
+            g.wait_ge(sem.relc, bits(topo.mask(cores[p], core)))
+            send(codes(T.mc[:, cols(so)]), codes(T.rc[:]), sem["arr%d" % so], cores[oo])
+        if plane_by[p] == rank:
+            g.wait_ge(sem.rels, bits(topo.mask(cores[p], core)))
+            send(T.ms[:, cols(so)], T.rs[:], sem["arr%d" % so], cores[oo])
+    g.wait_ge(sem.snd, sent[0])

@@ -1,8 +1,8 @@
 import numpy as np
-from concourse.bass import DstId, RemoteDMATransfer
 from concourse.mybir import dt, AluOpType, ActivationFunctionType
 
 W = 128
+PIECES = [("c", 0, 52, 0, 0), ("c", 52, 128, 0, 1), ("s", 0, 128, 1, 0)]
 SCRATCH = {
     "mc": ("sbuf", [128, 4 * W], "float8_e4m3fn_x4"),
     "ms": ("sbuf", [128, 4 * W], "uint8"),
@@ -21,8 +21,9 @@ SCRATCH = {
     "yt": ("sbuf", [128, 4 * W], "float32"),
     "ps": ("psum", [128, 2048], "float32"),
 }
-SEMAPHORES = (["ldk", "ldq", "zero", "iota", "diag", "sq", "scaled", "kq", "snd", "relc", "rels", "qq", "st"]
-              + ["mm%d" % i for i in range(4)] + ["arr%d" % i for i in range(4)] + ["cp%d" % i for i in range(4)])
+SEMAPHORES = (["ldk", "ldq", "zero", "iota", "diag", "scaled", "kq", "snd", "qq", "st"]
+              + ["rel%d" % i for i in range(len(PIECES))]
+              + ["%s%d" % (n, i) for n in ("sq", "mm", "arr", "cp") for i in range(4)])
 F = float(np.float32(0.8))
 
 
@@ -30,23 +31,26 @@ def plan(T, topo):
     own, cores = T.tables["OWN"], T.cores
     n = len(own)
     prods = {o: [p for p in range(n) if own[p] == o and p != o] for o in range(n) if own[o] == o}
-    codes_by, plane_by = {}, {}
+    relay = {}
     for o in prods:
         for p in prods[o]:
             a, b = cores[p], cores[o]
             if topo.may_write(a, b):
                 continue
             ok = [r for r in range(n) if own[r] != r and topo.may_write(a, cores[r]) and topo.may_write(cores[r], b)]
-            first = [r for r in ok if topo.chip(cores[r]) == topo.chip(a) and topo.same_plane(cores[r], b)]
-            second = [r for r in ok if topo.chip(cores[r]) == topo.chip(b) and topo.same_plane(a, cores[r])]
-            first, second = first or ok, second or ok
-            codes_by[p] = first[0]
-            plane_by[p] = second[0]
-    return prods, codes_by, plane_by
+            cable = [r for r in ok if topo.chip(cores[r]) == topo.chip(a) and topo.same_plane(cores[r], b)]
+            switch = [r for r in ok if topo.chip(cores[r]) == topo.chip(b) and topo.same_plane(a, cores[r])]
+            relay[p] = ((cable or ok)[0], (switch or ok)[0])
+    return prods, relay
 
 
 def bits(m):
     return bin(m).count("1")
+
+
+def turn(m, k):
+    on = [i for i in range(16) if m >> i & 1]
+    return sum(1 << i for i in on[k::2])
 
 
 def rank_program(g, core, T, topo):
@@ -54,7 +58,7 @@ def rank_program(g, core, T, topo):
     if rank is None:
         return
     own, cores, sem = T.tables["OWN"], T.cores, T.sem
-    prods, codes_by, plane_by = plan(T, topo)
+    prods, relay = plan(T, topo)
     slot = {p: 1 + i for o in prods for i, p in enumerate(prods[o])}
 
     def cols(b):
@@ -75,7 +79,7 @@ def rank_program(g, core, T, topo):
         g.tensor.wait_ge(sem.qq, 1)
 
         def lateness(p):
-            if p in codes_by:
+            if p in relay:
                 return 2
             return 0 if topo.rack(topo.host(cores[p])) == topo.rack(topo.host(core)) else 1
         order = [rank] + sorted(prods[rank], key=lateness)
@@ -84,9 +88,8 @@ def rank_program(g, core, T, topo):
             if p == rank:
                 g.tensor.wait_ge(sem.ldk, 32)
             else:
-                mc = topo.mask(cores[codes_by.get(p, p)], core)
-                ms = topo.mask(cores[plane_by.get(p, p)], core)
-                g.tensor.wait_ge(sem["arr%d" % s], bits(mc) + bits(ms))
+                via = [relay[p][x[3]] for x in PIECES] if p in relay else [p, p]
+                g.tensor.wait_ge(sem["arr%d" % s], sum(bits(topo.mask(cores[r], core)) for r in via))
             mm, cp = sem["mm%d" % s], sem["cp%d" % s]
             g.tensor.matmul_mx(bank(s), T.qc[:], T.qs[:], T.mc[:, cols(s)], T.ms[:, cols(s)], True, True).then_inc(mm, 1)
             if (len(order) - 1 - i) % 2 == 0:
@@ -111,10 +114,10 @@ def rank_program(g, core, T, topo):
     g.vector.tensor_scalar(T.z[:, 3:4 * W:4], T.ndiag[:], 0.0, None, AluOpType.is_equal).then_inc(sem.diag, 1)
     g.vector.wait_ge(sem.diag, 1)
     for b in range(4):
-        g.vector.quantize_mx(T.sc[:, cols(b)], T.ss[:, cols(b)], T.z[:, 3 - b:3 - b + 4 * W]).then_inc(sem.sq, 1)
-    g.tensor.wait_ge(sem.sq, 4)
+        g.vector.quantize_mx(T.sc[:, cols(b)], T.ss[:, cols(b)], T.z[:, 3 - b:3 - b + 4 * W]).then_inc(sem["sq%d" % b], 1)
     g.tensor.wait_ge(sem.ldk, 32)
     for b in range(4):
+        g.tensor.wait_ge(sem["sq%d" % b], 1)
         g.tensor.matmul_mx(bank(b), T.sc[:, cols(b)], T.ss[:, cols(b)], T.mc[:, cols(0)], T.ms[:, cols(0)],
                            True, True).then_inc(sem["mm%d" % b], 1)
     for b in range(4):
@@ -130,26 +133,33 @@ def rank_program(g, core, T, topo):
 
     sent = [0]
 
-    def send(out, in_, rsem, dst):
+    def send(out, in_, rsem, dst, m):
         rid, pid = topo.addr(dst, core)
-        m = topo.mask(core, dst)
         g.remote_dma(out, in_, rsem, sem.snd, pid, rid, m)
         sent[0] += bits(m)
 
     g.wait_ge(sem.kq, 1)
     s, o = slot[rank], own[rank]
-    if rank in codes_by:
-        send(codes(T.rc[:]), codes(T.nc[:]), sem.relc, cores[codes_by[rank]])
-        send(T.rs[:], T.ns[:], sem.rels, cores[plane_by[rank]])
+    if rank in relay:
+        for i, (what, a, b, way, k) in enumerate(PIECES):
+            d, r = cores[relay[rank][way]], sem["rel%d" % i]
+            m = turn(topo.mask(core, d), k)
+            if what == "c":
+                send(codes(T.rc[:, a:b]), codes(T.nc[:, a:b]), r, d, m)
+            else:
+                send(T.rs[:, a:b], T.ns[:, a:b], r, d, m)
     else:
-        send(codes(T.mc[:, cols(s)]), codes(T.nc[:]), sem["arr%d" % s], cores[o])
-        send(T.ms[:, cols(s)], T.ns[:], sem["arr%d" % s], cores[o])
-    for p in sorted(codes_by):
-        so, oo = slot[p], own[p]
-        if codes_by[p] == rank:
-            g.wait_ge(sem.relc, bits(topo.mask(cores[p], core)))
-            send(codes(T.mc[:, cols(so)]), codes(T.rc[:]), sem["arr%d" % so], cores[oo])
-        if plane_by[p] == rank:
-            g.wait_ge(sem.rels, bits(topo.mask(cores[p], core)))
-            send(T.ms[:, cols(so)], T.rs[:], sem["arr%d" % so], cores[oo])
+        d, arr = cores[o], sem["arr%d" % s]
+        send(codes(T.mc[:, cols(s)]), codes(T.nc[:]), arr, d, topo.mask(core, d))
+        send(T.ms[:, cols(s)], T.ns[:], arr, d, topo.mask(core, d))
+    for p in sorted(relay):
+        d, arr, c0 = cores[own[p]], sem["arr%d" % slot[p]], W * slot[p]
+        for i, (what, a, b, way, k) in enumerate(PIECES):
+            if relay[p][way] != rank:
+                continue
+            g.wait_ge(sem["rel%d" % i], bits(turn(topo.mask(cores[p], core), k)))
+            if what == "c":
+                send(codes(T.mc[:, c0 + a:c0 + b]), codes(T.rc[:, a:b]), arr, d, topo.mask(core, d))
+            else:
+                send(T.ms[:, c0 + a:c0 + b], T.rs[:, a:b], arr, d, topo.mask(core, d))
     g.wait_ge(sem.snd, sent[0])

import numpy as np
from concourse.mybir import dt, AluOpType, ActivationFunctionType

W = 128
PIECES = [("c", 0, 52, 0, 0), ("c", 52, 128, 0, 1), ("s", 0, 128, 1, 0)]
SCRATCH = {
    "mc": ("sbuf", [128, 4 * W], "float8_e4m3fn_x4"),
    "ms": ("sbuf", [128, 4 * W], "uint8"),
    "ndiag": ("sbuf", [128, W], "bfloat16"),
    "z": ("sbuf", [128, 4 * W + 4], "bfloat16"),
    "sc": ("sbuf", [128, 4 * W], "float8_e4m3fn_x4"),
    "ss": ("sbuf", [128, 4 * W], "uint8"),
    "kt": ("sbuf", [128, 4 * W], "bfloat16"),
    "nc": ("sbuf", [128, W], "float8_e4m3fn_x4"),
    "ns": ("sbuf", [128, W], "uint8"),
    "rc": ("sbuf", [128, W], "float8_e4m3fn_x4"),
    "rs": ("sbuf", [128, W], "uint8"),
    "qt": ("sbuf", [128, 4 * W], "bfloat16"),
    "qc": ("sbuf", [128, W], "float8_e4m3fn_x4"),
    "qs": ("sbuf", [128, W], "uint8"),
    "yt": ("sbuf", [128, 4 * W], "float32"),
    "ps": ("psum", [128, 2048], "float32"),
}
SEMAPHORES = (["ldk", "ldq", "zero", "iota", "diag", "scaled", "kq", "snd", "qq", "st"]
              + ["rel%d" % i for i in range(len(PIECES))]
              + ["%s%d" % (n, i) for n in ("sq", "mm", "arr", "cp") for i in range(4)])
F = float(np.float32(0.8))


def plan(T, topo):
    own, cores = T.tables["OWN"], T.cores
    n = len(own)
    prods = {o: [p for p in range(n) if own[p] == o and p != o] for o in range(n) if own[o] == o}
    relay = {}
    for o in prods:
        for p in prods[o]:
            a, b = cores[p], cores[o]
            if topo.may_write(a, b):
                continue
            ok = [r for r in range(n) if own[r] != r and topo.may_write(a, cores[r]) and topo.may_write(cores[r], b)]
            cable = [r for r in ok if topo.chip(cores[r]) == topo.chip(a) and topo.same_plane(cores[r], b)]
            switch = [r for r in ok if topo.chip(cores[r]) == topo.chip(b) and topo.same_plane(a, cores[r])]
            relay[p] = ((cable or ok)[0], (switch or ok)[0])
    return prods, relay


def bits(m):
    return bin(m).count("1")


def turn(m, k):
    on = [i for i in range(16) if m >> i & 1]
    return sum(1 << i for i in on[k::2])


def rank_program(g, core, T, topo):
    rank = T.rank_of(core)
    if rank is None:
        return
    own, cores, sem = T.tables["OWN"], T.cores, T.sem
    prods, relay = plan(T, topo)
    slot = {p: 1 + i for o in prods for i, p in enumerate(prods[o])}

    def cols(b):
        return slice(W * b, W * b + W)

    def bank(b):
        return T.ps[:, 512 * b:512 * b + W]

    def codes(ap):
        return ap.bitcast(dt.uint8)

    if own[rank] == rank:
        g.sync.dma_start(T.qt[:], T.q[:]).then_inc(sem.ldq, 16)
        g.scalar.dma_start(codes(T.mc[:, cols(0)]), T.kc[:]).then_inc(sem.ldk, 16)
        g.sync.dma_start(T.ms[:, cols(0)], T.ks[:]).then_inc(sem.ldk, 16)
        g.vector.wait_ge(sem.ldq, 16)
        g.vector.quantize_mx(T.qc[:], T.qs[:], T.qt[:]).then_inc(sem.qq, 1)
        g.tensor.wait_ge(sem.qq, 1)

        def lateness(p):
            if p in relay:
                return 2
            return 0 if topo.rack(topo.host(cores[p])) == topo.rack(topo.host(core)) else 1
        order = [rank] + sorted(prods[rank], key=lateness)
        for i, p in enumerate(order):
            s = 0 if p == rank else slot[p]
            if p == rank:
                g.tensor.wait_ge(sem.ldk, 32)
            else:
                via = [relay[p][x[3]] for x in PIECES] if p in relay else [p, p]
                g.tensor.wait_ge(sem["arr%d" % s], sum(bits(topo.mask(cores[r], core)) for r in via))
            mm, cp = sem["mm%d" % s], sem["cp%d" % s]
            g.tensor.matmul_mx(bank(s), T.qc[:], T.qs[:], T.mc[:, cols(s)], T.ms[:, cols(s)], True, True).then_inc(mm, 1)
            if (len(order) - 1 - i) % 2 == 0:
                g.vector.wait_ge(mm, 1)
                g.vector.tensor_copy(T.yt[:, cols(s)], bank(s)).then_inc(cp, 1)
                dq = g.sync
            else:
                g.scalar.wait_ge(mm, 1)
                g.scalar.activation(T.yt[:, cols(s)], bank(s), ActivationFunctionType.Copy).then_inc(cp, 1)
                dq = g.scalar
            dq.wait_ge(cp, 1)
            dq.dma_start(T.y[:, cols(s)], T.yt[:, cols(s)]).then_inc(sem.st, 16)
        g.sync.wait_ge(sem.st, 16 * len(order))
        return

    g.sync.dma_start(codes(T.mc[:, cols(0)]), T.kc[:]).then_inc(sem.ldk, 16)
    g.scalar.dma_start(T.ms[:, cols(0)], T.ks[:]).then_inc(sem.ldk, 16)
    g.iota(T.ndiag[:], [[1, W]], 0, -1, allow_small_or_imprecise_dtypes=True).then_inc(sem.iota, 1)
    g.vector.memset(T.z[:], 0.0).then_inc(sem.zero, 1)
    g.vector.wait_ge(sem.zero, 1)
    g.vector.wait_ge(sem.iota, 1)
    g.vector.tensor_scalar(T.z[:, 3:4 * W:4], T.ndiag[:], 0.0, None, AluOpType.is_equal).then_inc(sem.diag, 1)
    g.vector.wait_ge(sem.diag, 1)
    for b in range(4):
        g.vector.quantize_mx(T.sc[:, cols(b)], T.ss[:, cols(b)], T.z[:, 3 - b:3 - b + 4 * W]).then_inc(sem["sq%d" % b], 1)
    g.tensor.wait_ge(sem.ldk, 32)
    for b in range(4):
        g.tensor.wait_ge(sem["sq%d" % b], 1)
        g.tensor.matmul_mx(bank(b), T.sc[:, cols(b)], T.ss[:, cols(b)], T.mc[:, cols(0)], T.ms[:, cols(0)],
                           True, True).then_inc(sem["mm%d" % b], 1)
    for b in range(4):
        out = T.kt[:, b:4 * W:4]
        if b % 2 == 0:
            g.scalar.wait_ge(sem["mm%d" % b], 1)
            g.scalar.activation(out, bank(b), ActivationFunctionType.Copy, scale=F).then_inc(sem.scaled, 1)
        else:
            g.vector.wait_ge(sem["mm%d" % b], 1)
            g.vector.tensor_scalar(out, bank(b), F, None, AluOpType.mult).then_inc(sem.scaled, 1)
    g.vector.wait_ge(sem.scaled, 4)
    g.vector.quantize_mx(T.nc[:], T.ns[:], T.kt[:]).then_inc(sem.kq, 1)

    sent = [0]

    def send(out, in_, rsem, dst, m):
        rid, pid = topo.addr(dst, core)
        g.remote_dma(out, in_, rsem, sem.snd, pid, rid, m)
        sent[0] += bits(m)

    g.wait_ge(sem.kq, 1)
    s, o = slot[rank], own[rank]
    if rank in relay:
        for i, (what, a, b, way, k) in enumerate(PIECES):
            d, r = cores[relay[rank][way]], sem["rel%d" % i]
            m = turn(topo.mask(core, d), k)
            if what == "c":
                send(codes(T.rc[:, a:b]), codes(T.nc[:, a:b]), r, d, m)
            else:
                send(T.rs[:, a:b], T.ns[:, a:b], r, d, m)
    else:
        d, arr = cores[o], sem["arr%d" % s]
        send(codes(T.mc[:, cols(s)]), codes(T.nc[:]), arr, d, topo.mask(core, d))
        send(T.ms[:, cols(s)], T.ns[:], arr, d, topo.mask(core, d))
    for p in sorted(relay):
        d, arr, c0 = cores[own[p]], sem["arr%d" % slot[p]], W * slot[p]
        for i, (what, a, b, way, k) in enumerate(PIECES):
            if relay[p][way] != rank:
                continue
            g.wait_ge(sem["rel%d" % i], bits(turn(topo.mask(cores[p], core), k)))
            if what == "c":
                send(codes(T.mc[:, c0 + a:c0 + b]), codes(T.rc[:, a:b]), arr, d, topo.mask(core, d))
            else:
                send(T.ms[:, c0 + a:c0 + b], T.rs[:, a:b], arr, d, topo.mask(core, d))
    g.wait_ge(sem.snd, sent[0])
